import numpy as np
import ml_dtypes


def mxq(x, axis, fmt="e4m3"):
    dtype, down = {"e4m3": (ml_dtypes.float8_e4m3fn, 7), "e5m2": (ml_dtypes.float8_e5m2, 14)}[fmt]
    v = np.moveaxis(np.asarray(x, np.float32).astype(ml_dtypes.bfloat16).astype(np.float64), axis, -1)
    blocks = v.reshape(v.shape[:-1] + (-1, 32))
    amax = np.abs(blocks).max(-1, keepdims=True)
    byte = np.maximum(np.where(amax > 0, np.frexp(amax)[1] - 1 + 127, 0) - down, 1)
    scale = np.exp2(byte - 127.0)
    codes = (blocks / scale).astype(np.float32).astype(dtype).astype(np.float64)
    return np.moveaxis((codes * scale).reshape(v.shape), -1, axis)


WIDE = False


def mx_kscale(k):
    if not WIDE:
        return np.ones(k)
    levels = np.array([10, -10, 5, -5, 0])
    if k % 512:
        return np.exp2(np.random.permutation(np.resize(levels, k // 32))).repeat(32)
    a = np.empty((k // 512, 16))
    for p in range(k // 512):
        a[p, :8] = np.random.permutation(np.resize(levels, 8))
        for g in range(8):
            far = levels[np.abs(levels - a[p, g]) >= 10]
            a[p, g + 8] = far[np.random.randint(len(far))]
    return np.exp2(a.ravel()).repeat(32)


def f64(x):
    return np.asarray(x).astype(np.float64)


def striped(idx):
    return np.tile(idx.reshape(-1, 16).T, (8, 1)).astype(np.uint16)


def unstriped(offs):
    return offs[:16].T.reshape(-1).astype(np.int64)


K, T, E, C, N = 512, 512, 4, 128, 512


def by_expert(wq, xq):
    return np.concatenate([wq[e].T @ xq[:, e * C:(e + 1) * C] for e in range(E)], axis=1)


def setup_inputs():
    n = np.random.standard_normal
    s = mx_kscale(K)[:, None]
    return {
        "xT": (n((K, T)) * s).astype(np.float32),
        "w": (n((E, K, N)) / np.sqrt(K) / s[None]).astype(np.float32),
        "gate": np.tile(np.random.uniform(0.2, 1.0, E * C), (N, 1)).astype(np.float32),
        "offs": striped(np.random.permutation(T)[:E * C]),
    }


def reference(xT, w, gate, offs):
    idx = unstriped(offs)
    xq = mxq(f64(xT)[:, idx], 0, "e4m3")
    y = by_expert(mxq(f64(w), 1, "e4m3"), xq)
    out = np.zeros((N, T))
    out[:, idx] = f64(gate) * y
    return out

@@ -1,0 +1,134 @@
+from contextlib import ExitStack
+
+import concourse.mybir as mybir
+
+K, T, E, C, N = 512, 512, 4, 128, 512
+FLOPS = 2 * K * N * E * C
+
+F32 = mybir.dt.float32
+BF16 = mybir.dt.bfloat16
+U32 = mybir.dt.uint32
+U16 = mybir.dt.uint16
+U8 = mybir.dt.uint8
+FP8X4 = mybir.dt.float8_e4m3fn_x4
+MULT = mybir.AluOpType.mult
+
+P = 128
+PACK = 4
+NB = N // P
+S = E * C
+HALF = 256
+
+
+def tile_routed_moe_kernel(tc, xT, w, gate, offs, out):
+    nc = tc.nc
+    with ExitStack() as ctx:
+        lists = ctx.enter_context(tc.tile_pool(name="lists", bufs=1))
+        keep = ctx.enter_context(tc.tile_pool(name="keep", bufs=1))
+        psum = ctx.enter_context(tc.psum_pool(name="psum", bufs=1))
+
+        offsets = lists.tile([P, S // 16], U16, name="offsets")
+        nc.sync.dma_start(offsets[:], offs)
+
+        x_view = xT.rearrange("(p t) n -> p t n", t=PACK)
+        planes = []
+        for t in range(PACK):
+            plane = keep.tile([P, T], F32, name="plane%d" % t)
+            nc.sync.dma_start(plane[:], x_view[:, t, :])
+            planes.append(plane)
+
+        w_view = w.rearrange("e (p t) n -> e p t n", t=PACK)
+        w_raw = []
+        gate_sb = keep.tile([P, NB, S], F32, name="gate_sb")
+        for e in range(E):
+            raw = keep.tile([P, PACK, N], F32, name="w_raw%d" % e)
+            nc.sync.dma_start(raw[:], w_view[e])
+            w_raw.append(raw)
+            if e == 1:
+                nc.sync.dma_start(gate_sb[:], gate.rearrange("(b p) j -> p b j", p=P))
+
+        x_codes = keep.tile([P, S], U32, name="x_codes", align_bytes=64)
+        x_scales = keep.tile([P, S], U8, name="x_scales", align_bytes=64)
+        y_all = keep.tile([P, NB, S], F32, name="y_all")
+        windows = [keep.tile([P, T], F32, name="window%d" % b) for b in range(NB)]
+
+        x_grouped = []
+        g4s = []
+        for h in range(2):
+            g4 = keep.tile([P, PACK, HALF], F32, name="g4_%d" % h)
+            for t in range(PACK):
+                nc.vector.tensor_copy(
+                    g4[:, t, :], planes[t][:].indirect(offsets[:, h * (HALF // 16) : (h + 1) * (HALF // 16)])
+                )
+            g4s.append(g4)
+            xg = keep.tile([P, HALF, PACK], BF16, name="xg%d" % h, align_bytes=64)
+            x_grouped.append(xg)
+            if h == 0:
+                nc.scalar.copy(out=xg[:], in_=g4[:].rearrange("p t c -> p c t"))
+
+        w_grouped = [keep.tile([P, N, PACK], BF16, name="wg%d" % e, align_bytes=64) for e in range(E)]
+        w_codes = [keep.tile([P, N], U32, name="w_codes%d" % e, align_bytes=64) for e in range(E)]
+        w_scales = [keep.tile([P, N], U8, name="w_scales%d" % e, align_bytes=64) for e in range(E)]
+
+        def interleave_w(engine_copy, e, c0, c1):
+            engine_copy(out=w_grouped[e][:, c0:c1, :], in_=w_raw[e][:, :, c0:c1].rearrange("p t n -> p n t"))
+
+        def quantize_w(e):
+            nc.vector.quantize_mx(
+                out=w_codes[e][:].bitcast(FP8X4),
+                scales=w_scales[e][:],
+                in_=w_grouped[e][:].rearrange("p n t -> p (n t)"),
+            )
+
+        def quantize_x(h):
+            cols = slice(h * HALF, (h + 1) * HALF)
+            nc.vector.quantize_mx(
+                out=x_codes[:, cols].bitcast(FP8X4),
+                scales=x_scales[:, cols],
+                in_=x_grouped[h][:].rearrange("p c t -> p (c t)"),
+            )
+
+        def multiply(e):
+            acc = psum.tile([P, NB, C], F32, name="acc%d" % e)
+            slots = slice(e * C, (e + 1) * C)
+            for b in range(NB):
+                feats = slice(b * P, (b + 1) * P)
+                nc.tensor.matmul_mx(
+                    out=acc[:, b, :],
+                    lhsT=w_codes[e][:, feats].bitcast(FP8X4),
+                    lhsT_scale=w_scales[e][:, feats],
+                    rhs=x_codes[:, slots].bitcast(FP8X4),
+                    rhs_scale=x_scales[:, slots],
+                    start=True,
+                    stop=True,
+                )
+            nc.vector.tensor_tensor(out=y_all[:, :, slots], in0=acc[:], in1=gate_sb[:, :, slots], op=MULT)
+
+        def scatter(b, s0, s1):
+            nc.vector.tensor_copy(windows[b][:].indirect(offsets[:, s0 // 16 : s1 // 16]), y_all[:, b, s0:s1])
+
+        interleave_w(nc.scalar.copy, 0, 0, N // 2)
+        interleave_w(nc.vector.tensor_copy, 0, N // 2, N)
+        nc.vector.tensor_copy(out=x_grouped[1][:], in_=g4s[1][:].rearrange("p t c -> p c t"))
+        quantize_x(0)
+        quantize_w(0)
+        quantize_x(1)
+        multiply(0)
+        interleave_w(nc.scalar.copy, 1, 0, N)
+        for b in range(NB):
+            scatter(b, 0, C)
+        quantize_w(1)
+        multiply(1)
+        interleave_w(nc.scalar.copy, 2, 0, N)
+        for b in range(NB):
+            scatter(b, C, 2 * C)
+        quantize_w(2)
+        multiply(2)
+        interleave_w(nc.scalar.copy, 3, 0, N)
+        for b in range(NB):
+            scatter(b, 2 * C, 3 * C)
+        quantize_w(3)
+        multiply(3)
+        for b in range(NB):
+            scatter(b, 3 * C, 4 * C)
+            nc.sync.dma_start(out[b * P : (b + 1) * P, :], windows[b][:])

@@ -12,6 +12,7 @@ U16 = mybir.dt.uint16
 U8 = mybir.dt.uint8
 FP8X4 = mybir.dt.float8_e4m3fn_x4
 MULT = mybir.AluOpType.mult
+ADD = mybir.AluOpType.add
 
 P = 128
 PACK = 4
@@ -38,37 +39,36 @@ def tile_routed_moe_kernel(tc, xT, w, gate, offs, out):
             planes.append(plane)
 
         w_view = w.rearrange("e (p t) n -> e p t n", t=PACK)
-        w_raw = []
-        gate_sb = keep.tile([P, NB, S], F32, name="gate_sb")
-        for e in range(E):
-            raw = keep.tile([P, PACK, N], F32, name="w_raw%d" % e)
-            nc.sync.dma_start(raw[:], w_view[e])
-            w_raw.append(raw)
-            if e == 1:
-                nc.sync.dma_start(gate_sb[:], gate.rearrange("(b p) j -> p b j", p=P))
+        gate_view = gate.rearrange("(b p) j -> p b j", p=P)
+        w_raw = [keep.tile([P, PACK, N], F32, name="w_raw%d" % e, tag="raw%d" % e) for e in range(E)]
+        gate_sb = [keep.tile([P, NB, HALF], F32, name="gate_sb%d" % h) for h in range(2)]
+        nc.sync.dma_start(w_raw[0][:], w_view[0])
+        nc.sync.dma_start(gate_sb[0][:], gate_view[:, :, 0:HALF])
+        nc.sync.dma_start(w_raw[1][:], w_view[1])
+        nc.sync.dma_start(w_raw[2][:], w_view[2])
+        nc.sync.dma_start(w_raw[3][:], w_view[3])
+        nc.sync.dma_start(gate_sb[1][:], gate_view[:, :, HALF:S])
 
         x_codes = keep.tile([P, S], U32, name="x_codes", align_bytes=64)
         x_scales = keep.tile([P, S], U8, name="x_scales", align_bytes=64)
         y_all = keep.tile([P, NB, S], F32, name="y_all")
         windows = [keep.tile([P, T], F32, name="window%d" % b) for b in range(NB)]
-
-        x_grouped = []
-        g4s = []
-        for h in range(2):
-            g4 = keep.tile([P, PACK, HALF], F32, name="g4_%d" % h)
-            for t in range(PACK):
-                nc.vector.tensor_copy(
-                    g4[:, t, :], planes[t][:].indirect(offsets[:, h * (HALF // 16) : (h + 1) * (HALF // 16)])
-                )
-            g4s.append(g4)
-            xg = keep.tile([P, HALF, PACK], BF16, name="xg%d" % h, align_bytes=64)
-            x_grouped.append(xg)
-            if h == 0:
-                nc.scalar.copy(out=xg[:], in_=g4[:].rearrange("p t c -> p c t"))
-
+        g4s = [keep.tile([P, PACK, HALF], F32, name="g4_%d" % h) for h in range(2)]
+        x_grouped = [keep.tile([P, HALF, PACK], BF16, name="xg%d" % h, align_bytes=64) for h in range(2)]
         w_grouped = [keep.tile([P, N, PACK], BF16, name="wg%d" % e, align_bytes=64) for e in range(E)]
         w_codes = [keep.tile([P, N], U32, name="w_codes%d" % e, align_bytes=64) for e in range(E)]
         w_scales = [keep.tile([P, N], U8, name="w_scales%d" % e, align_bytes=64) for e in range(E)]
+        accs = [psum.tile([P, NB, C], F32, name="acc%d" % e) for e in range(E)]
+        y_raws = {}
+
+        def gather(h):
+            for t in range(PACK):
+                nc.vector.tensor_copy(
+                    g4s[h][:, t, :], planes[t][:].indirect(offsets[:, h * (HALF // 16) : (h + 1) * (HALF // 16)])
+                )
+
+        def interleave_x(engine_copy, h):
+            engine_copy(out=x_grouped[h][:], in_=g4s[h][:].rearrange("p t c -> p c t"))
 
         def interleave_w(engine_copy, e, c0, c1):
             engine_copy(out=w_grouped[e][:, c0:c1, :], in_=w_raw[e][:, :, c0:c1].rearrange("p t n -> p n t"))
@@ -89,12 +89,11 @@ def tile_routed_moe_kernel(tc, xT, w, gate, offs, out):
             )
 
         def multiply(e):
-            acc = psum.tile([P, NB, C], F32, name="acc%d" % e)
             slots = slice(e * C, (e + 1) * C)
             for b in range(NB):
                 feats = slice(b * P, (b + 1) * P)
                 nc.tensor.matmul_mx(
-                    out=acc[:, b, :],
+                    out=accs[e][:, b, :],
                     lhsT=w_codes[e][:, feats].bitcast(FP8X4),
                     lhsT_scale=w_scales[e][:, feats],
                     rhs=x_codes[:, slots].bitcast(FP8X4),
@@ -102,33 +101,68 @@ def tile_routed_moe_kernel(tc, xT, w, gate, offs, out):
                     start=True,
                     stop=True,
                 )
-            nc.vector.tensor_tensor(out=y_all[:, :, slots], in0=acc[:], in1=gate_sb[:, :, slots], op=MULT)
 
-        def scatter(b, s0, s1):
-            nc.vector.tensor_copy(windows[b][:].indirect(offsets[:, s0 // 16 : s1 // 16]), y_all[:, b, s0:s1])
+        def gate_of(e):
+            return gate_sb[e // 2][:, :, (e % 2) * C : (e % 2 + 1) * C]
 
-        interleave_w(nc.scalar.copy, 0, 0, N // 2)
-        interleave_w(nc.vector.tensor_copy, 0, N // 2, N)
-        nc.vector.tensor_copy(out=x_grouped[1][:], in_=g4s[1][:].rearrange("p t c -> p c t"))
+        def slots_of(e):
+            return slice(e * C, (e + 1) * C)
+
+        def weigh_on_vector(e):
+            nc.vector.tensor_tensor(out=y_all[:, :, slots_of(e)], in0=accs[e][:], in1=gate_of(e), op=MULT)
+
+        def empty_bank(e, tag):
+            y_raw = keep.tile([P, NB, C], F32, name="y_raw%d" % e, tag=tag)
+            nc.scalar.copy(out=y_raw[:], in_=accs[e][:])
+            y_raws[e] = y_raw
+
+        def offsets_of(e):
+            return offsets[:, e * (C // 16) : (e + 1) * (C // 16)]
+
+        def scatter_weighed(e, b):
+            nc.vector.tensor_copy(windows[b][:].indirect(offsets_of(e)), y_all[:, b, slots_of(e)])
+
+        def weigh_and_scatter(e, b):
+            nc.vector.tensor_tensor(
+                out=windows[b][:].indirect(offsets_of(e)), in0=y_raws[e][:, b, :], in1=gate_of(e)[:, b, :], op=MULT
+            )
+
+        H = N // 2
+        gather(0)
+        interleave_x(nc.scalar.copy, 0)
+        gather(1)
+        interleave_w(nc.scalar.copy, 0, 0, H)
+        interleave_w(nc.vector.tensor_copy, 0, H, N)
         quantize_x(0)
         quantize_w(0)
-        quantize_x(1)
         multiply(0)
-        interleave_w(nc.scalar.copy, 1, 0, N)
-        for b in range(NB):
-            scatter(b, 0, C)
+        interleave_x(nc.vector.tensor_copy, 1)
+        quantize_x(1)
+        interleave_w(nc.scalar.copy, 1, 0, H)
+        interleave_w(nc.scalar.copy, 1, H, N)
+        weigh_on_vector(0)
+        scatter_weighed(0, 0)
         quantize_w(1)
         multiply(1)
-        interleave_w(nc.scalar.copy, 2, 0, N)
-        for b in range(NB):
-            scatter(b, C, 2 * C)
+        interleave_w(nc.scalar.copy, 2, 0, H)
+        interleave_w(nc.scalar.copy, 2, H, N)
+        empty_bank(1, "raw2")
+        scatter_weighed(0, 1)
+        scatter_weighed(0, 2)
         quantize_w(2)
         multiply(2)
-        interleave_w(nc.scalar.copy, 3, 0, N)
-        for b in range(NB):
-            scatter(b, 2 * C, 3 * C)
+        interleave_w(nc.scalar.copy, 3, 0, H)
+        interleave_w(nc.scalar.copy, 3, H, N)
+        empty_bank(2, "raw3")
+        scatter_weighed(0, 3)
+        weigh_and_scatter(1, 0)
         quantize_w(3)
         multiply(3)
+        empty_bank(3, "raw0")
+        for b in (1, 2, 3):
+            weigh_and_scatter(1, b)
         for b in range(NB):
-            scatter(b, 3 * C, 4 * C)
+            weigh_and_scatter(2, b)
+        for b in range(NB):
+            weigh_and_scatter(3, b)
             nc.sync.dma_start(out[b * P : (b + 1) * P, :], windows[b][:])

@@ -42,7 +42,8 @@ def tile_routed_moe_kernel(tc, xT, w, gate, offs, out):
         gate_view = gate.rearrange("(b p) j -> p b j", p=P)
         w_raw = [keep.tile([P, PACK, N], F32, name="w_raw%d" % e, tag="raw%d" % e) for e in range(E)]
         gate_sb = [keep.tile([P, NB, HALF], F32, name="gate_sb%d" % h) for h in range(2)]
-        nc.sync.dma_start(w_raw[0][:], w_view[0])
+        for t in range(PACK):
+            nc.sync.dma_start(w_raw[0][:, t, :], w_view[0][:, t, :])
         nc.sync.dma_start(gate_sb[0][:], gate_view[:, :, 0:HALF])
         nc.sync.dma_start(w_raw[1][:], w_view[1])
         nc.sync.dma_start(w_raw[2][:], w_view[2])
@@ -51,14 +52,15 @@ def tile_routed_moe_kernel(tc, xT, w, gate, offs, out):
 
         x_codes = keep.tile([P, S], U32, name="x_codes", align_bytes=64)
         x_scales = keep.tile([P, S], U8, name="x_scales", align_bytes=64)
-        y_all = keep.tile([P, NB, S], F32, name="y_all")
+        y_first = [keep.tile([P, NB // 2, C], F32, name="y_first%d" % u) for u in range(2)]
+        acc_first = [psum.tile([P, NB // 2, C], F32, name="acc_first%d" % u) for u in range(2)]
         windows = [keep.tile([P, T], F32, name="window%d" % b) for b in range(NB)]
         g4s = [keep.tile([P, PACK, HALF], F32, name="g4_%d" % h) for h in range(2)]
         x_grouped = [keep.tile([P, HALF, PACK], BF16, name="xg%d" % h, align_bytes=64) for h in range(2)]
         w_grouped = [keep.tile([P, N, PACK], BF16, name="wg%d" % e, align_bytes=64) for e in range(E)]
         w_codes = [keep.tile([P, N], U32, name="w_codes%d" % e, align_bytes=64) for e in range(E)]
         w_scales = [keep.tile([P, N], U8, name="w_scales%d" % e, align_bytes=64) for e in range(E)]
-        accs = [psum.tile([P, NB, C], F32, name="acc%d" % e) for e in range(E)]
+        accs = [None] + [psum.tile([P, NB, C], F32, name="acc%d" % e) for e in range(1, E)]
         y_raws = {}
 
         def gather(h):
@@ -73,11 +75,11 @@ def tile_routed_moe_kernel(tc, xT, w, gate, offs, out):
         def interleave_w(engine_copy, e, c0, c1):
             engine_copy(out=w_grouped[e][:, c0:c1, :], in_=w_raw[e][:, :, c0:c1].rearrange("p t n -> p n t"))
 
-        def quantize_w(e):
+        def quantize_w(e, c0=0, c1=N):
             nc.vector.quantize_mx(
-                out=w_codes[e][:].bitcast(FP8X4),
-                scales=w_scales[e][:],
-                in_=w_grouped[e][:].rearrange("p n t -> p (n t)"),
+                out=w_codes[e][:, c0:c1].bitcast(FP8X4),
+                scales=w_scales[e][:, c0:c1],
+                in_=w_grouped[e][:, c0:c1, :].rearrange("p n t -> p (n t)"),
             )
 
         def quantize_x(h):
@@ -88,12 +90,12 @@ def tile_routed_moe_kernel(tc, xT, w, gate, offs, out):
                 in_=x_grouped[h][:].rearrange("p c t -> p (c t)"),
             )
 
-        def multiply(e):
+        def multiply(e, blocks=(0, 1, 2, 3)):
             slots = slice(e * C, (e + 1) * C)
-            for b in range(NB):
+            for b in blocks:
                 feats = slice(b * P, (b + 1) * P)
                 nc.tensor.matmul_mx(
-                    out=accs[e][:, b, :],
+                    out=accs[e][:, b, :] if e > 0 else acc_first[b // 2][:, b % 2, :],
                     lhsT=w_codes[e][:, feats].bitcast(FP8X4),
                     lhsT_scale=w_scales[e][:, feats],
                     rhs=x_codes[:, slots].bitcast(FP8X4),
@@ -108,8 +110,10 @@ def tile_routed_moe_kernel(tc, xT, w, gate, offs, out):
         def slots_of(e):
             return slice(e * C, (e + 1) * C)
 
-        def weigh_on_vector(e):
-            nc.vector.tensor_tensor(out=y_all[:, :, slots_of(e)], in0=accs[e][:], in1=gate_of(e), op=MULT)
+        def weigh_first(u):
+            nc.vector.tensor_tensor(
+                out=y_first[u][:], in0=acc_first[u][:], in1=gate_of(0)[:, 2 * u : 2 * u + 2, :], op=MULT
+            )
 
         def empty_bank(e, tag):
             y_raw = keep.tile([P, NB, C], F32, name="y_raw%d" % e, tag=tag)
@@ -120,7 +124,7 @@ def tile_routed_moe_kernel(tc, xT, w, gate, offs, out):
             return offsets[:, e * (C // 16) : (e + 1) * (C // 16)]
 
         def scatter_weighed(e, b):
-            nc.vector.tensor_copy(windows[b][:].indirect(offsets_of(e)), y_all[:, b, slots_of(e)])
+            nc.vector.tensor_copy(windows[b][:].indirect(offsets_of(e)), y_first[b // 2][:, b % 2, :])
 
         def weigh_and_scatter(e, b):
             nc.vector.tensor_tensor(
@@ -131,23 +135,26 @@ def tile_routed_moe_kernel(tc, xT, w, gate, offs, out):
         gather(0)
         interleave_x(nc.scalar.copy, 0)
         gather(1)
-        interleave_w(nc.scalar.copy, 0, 0, H)
-        interleave_w(nc.vector.tensor_copy, 0, H, N)
+        interleave_w(nc.vector.tensor_copy, 0, 0, H)
         quantize_x(0)
-        quantize_w(0)
-        multiply(0)
-        interleave_x(nc.vector.tensor_copy, 1)
+        interleave_w(nc.vector.tensor_copy, 0, H, N)
+        quantize_w(0, 0, H)
+        multiply(0, (0, 1))
+        quantize_w(0, H, N)
+        multiply(0, (2, 3))
+        interleave_x(nc.scalar.copy, 1)
         quantize_x(1)
         interleave_w(nc.scalar.copy, 1, 0, H)
         interleave_w(nc.scalar.copy, 1, H, N)
-        weigh_on_vector(0)
+        weigh_first(0)
         scatter_weighed(0, 0)
+        weigh_first(1)
+        scatter_weighed(0, 1)
         quantize_w(1)
         multiply(1)
         interleave_w(nc.scalar.copy, 2, 0, H)
         interleave_w(nc.scalar.copy, 2, H, N)
         empty_bank(1, "raw2")
-        scatter_weighed(0, 1)
         scatter_weighed(0, 2)
         quantize_w(2)
         multiply(2)

@@ -70,10 +70,16 @@ def tile_routed_moe_kernel(tc, xT, w, gate, offs, out):
                 )
 
         def interleave_x(engine_copy, h):
-            engine_copy(out=x_grouped[h][:], in_=g4s[h][:].rearrange("p t c -> p c t"))
+            engine_copy(
+                out=x_grouped[h][:].rearrange("p (c i) t -> p c t i", i=4),
+                in_=g4s[h][:].rearrange("p t (c i) -> p c t i", i=4),
+            )
 
         def interleave_w(engine_copy, e, c0, c1):
-            engine_copy(out=w_grouped[e][:, c0:c1, :], in_=w_raw[e][:, :, c0:c1].rearrange("p t n -> p n t"))
+            engine_copy(
+                out=w_grouped[e][:, c0:c1, :].rearrange("p (c i) t -> p c t i", i=4),
+                in_=w_raw[e][:, :, c0:c1].rearrange("p t (c i) -> p c t i", i=4),
+            )
 
         def quantize_w(e, c0=0, c1=N):
             nc.vector.quantize_mx(

@@ -19,6 +19,8 @@ PACK = 4
 NB = N // P
 S = E * C
 HALF = 256
+H = N // 2
+UNITS = 2 * E
 
 
 def tile_routed_moe_kernel(tc, xT, w, gate, offs, out):
@@ -41,27 +43,27 @@ def tile_routed_moe_kernel(tc, xT, w, gate, offs, out):
         w_view = w.rearrange("e (p t) n -> e p t n", t=PACK)
         gate_view = gate.rearrange("(b p) j -> p b j", p=P)
         w_raw = [keep.tile([P, PACK, N], F32, name="w_raw%d" % e, tag="raw%d" % e) for e in range(E)]
-        gate_sb = [keep.tile([P, NB, HALF], F32, name="gate_sb%d" % h) for h in range(2)]
+        gate_a = [keep.tile([P, NB, C], F32, name="gate_a%d" % e) for e in range(2)]
+        gate_b = keep.tile([P, NB, HALF], F32, name="gate_b")
         for t in range(PACK):
             nc.sync.dma_start(w_raw[0][:, t, :], w_view[0][:, t, :])
-        nc.sync.dma_start(gate_sb[0][:], gate_view[:, :, 0:HALF])
+        nc.sync.dma_start(gate_a[0][:], gate_view[:, :, 0:C])
         nc.sync.dma_start(w_raw[1][:], w_view[1])
         nc.sync.dma_start(w_raw[2][:], w_view[2])
+        nc.sync.dma_start(gate_a[1][:], gate_view[:, :, C : 2 * C])
         nc.sync.dma_start(w_raw[3][:], w_view[3])
-        nc.sync.dma_start(gate_sb[1][:], gate_view[:, :, HALF:S])
+        nc.sync.dma_start(gate_b[:], gate_view[:, :, HALF:S])
 
-        x_codes = keep.tile([P, S], U32, name="x_codes", align_bytes=64)
-        x_scales = keep.tile([P, S], U8, name="x_scales", align_bytes=64)
-        y_first = [keep.tile([P, NB // 2, C], F32, name="y_first%d" % u) for u in range(2)]
-        acc_first = [psum.tile([P, NB // 2, C], F32, name="acc_first%d" % u) for u in range(2)]
+        x_codes = [keep.tile([P, HALF], U32, name="x_codes%d" % h, align_bytes=64) for h in range(2)]
+        x_scales = [keep.tile([P, HALF], U8, name="x_scales%d" % h, align_bytes=64) for h in range(2)]
         windows = [keep.tile([P, T], F32, name="window%d" % b) for b in range(NB)]
         g4s = [keep.tile([P, PACK, HALF], F32, name="g4_%d" % h) for h in range(2)]
-        x_grouped = [keep.tile([P, HALF, PACK], BF16, name="xg%d" % h, align_bytes=64) for h in range(2)]
-        w_grouped = [keep.tile([P, N, PACK], BF16, name="wg%d" % e, align_bytes=64) for e in range(E)]
-        w_codes = [keep.tile([P, N], U32, name="w_codes%d" % e, align_bytes=64) for e in range(E)]
-        w_scales = [keep.tile([P, N], U8, name="w_scales%d" % e, align_bytes=64) for e in range(E)]
-        accs = [None] + [psum.tile([P, NB, C], F32, name="acc%d" % e) for e in range(1, E)]
-        y_raws = {}
+        w_codes = [keep.tile([P, H], U32, name="w_codes%d" % u, align_bytes=64) for u in range(UNITS)]
+        w_scales = [keep.tile([P, H], U8, name="w_scales%d" % u, align_bytes=64) for u in range(UNITS)]
+        accs = [psum.tile([P, 2, C], F32, name="acc%d" % u) for u in range(UNITS)]
+        x_grouped = {}
+        w_grouped = {}
+        ys = {}
 
         def gather(h):
             for t in range(PACK):
@@ -69,113 +71,103 @@ def tile_routed_moe_kernel(tc, xT, w, gate, offs, out):
                     g4s[h][:, t, :], planes[t][:].indirect(offsets[:, h * (HALF // 16) : (h + 1) * (HALF // 16)])
                 )
 
-        def interleave_x(engine_copy, h):
+        def interleave_x(engine_copy, h, tag):
+            x_grouped[h] = keep.tile([P, HALF, PACK], BF16, name="xg%d" % h, tag=tag, align_bytes=64)
             engine_copy(
                 out=x_grouped[h][:].rearrange("p (c i) t -> p c t i", i=4),
                 in_=g4s[h][:].rearrange("p t (c i) -> p c t i", i=4),
             )
 
-        def interleave_w(engine_copy, e, c0, c1):
+        def interleave_w(engine_copy, u, tag):
+            e, c0 = u // 2, (u % 2) * H
+            w_grouped[u] = keep.tile([P, H, PACK], BF16, name="wg%d" % u, tag=tag, align_bytes=64)
             engine_copy(
-                out=w_grouped[e][:, c0:c1, :].rearrange("p (c i) t -> p c t i", i=4),
-                in_=w_raw[e][:, :, c0:c1].rearrange("p t (c i) -> p c t i", i=4),
+                out=w_grouped[u][:].rearrange("p (c i) t -> p c t i", i=4),
+                in_=w_raw[e][:, :, c0 : c0 + H].rearrange("p t (c i) -> p c t i", i=4),
             )
 
-        def quantize_w(e, c0=0, c1=N):
+        def quantize_w(u):
             nc.vector.quantize_mx(
-                out=w_codes[e][:, c0:c1].bitcast(FP8X4),
-                scales=w_scales[e][:, c0:c1],
-                in_=w_grouped[e][:, c0:c1, :].rearrange("p n t -> p (n t)"),
+                out=w_codes[u][:].bitcast(FP8X4),
+                scales=w_scales[u][:],
+                in_=w_grouped[u][:].rearrange("p n t -> p (n t)"),
             )
 
         def quantize_x(h):
-            cols = slice(h * HALF, (h + 1) * HALF)
             nc.vector.quantize_mx(
-                out=x_codes[:, cols].bitcast(FP8X4),
-                scales=x_scales[:, cols],
+                out=x_codes[h][:].bitcast(FP8X4),
+                scales=x_scales[h][:],
                 in_=x_grouped[h][:].rearrange("p c t -> p (c t)"),
             )
 
-        def multiply(e, blocks=(0, 1, 2, 3)):
-            slots = slice(e * C, (e + 1) * C)
-            for b in blocks:
-                feats = slice(b * P, (b + 1) * P)
+        def multiply(u):
+            e = u // 2
+            slots = slice((e % 2) * C, (e % 2 + 1) * C)
+            for i in range(2):
+                feats = slice(i * P, (i + 1) * P)
                 nc.tensor.matmul_mx(
-                    out=accs[e][:, b, :] if e > 0 else acc_first[b // 2][:, b % 2, :],
-                    lhsT=w_codes[e][:, feats].bitcast(FP8X4),
-                    lhsT_scale=w_scales[e][:, feats],
-                    rhs=x_codes[:, slots].bitcast(FP8X4),
-                    rhs_scale=x_scales[:, slots],
+                    out=accs[u][:, i, :],
+                    lhsT=w_codes[u][:, feats].bitcast(FP8X4),
+                    lhsT_scale=w_scales[u][:, feats],
+                    rhs=x_codes[e // 2][:, slots].bitcast(FP8X4),
+                    rhs_scale=x_scales[e // 2][:, slots],
                     start=True,
                     stop=True,
                 )
 
-        def gate_of(e):
-            return gate_sb[e // 2][:, :, (e % 2) * C : (e % 2 + 1) * C]
+        def gate_of(e, b):
+            if e < 2:
+                return gate_a[e][:, b, :]
+            return gate_b[:, b, (e - 2) * C : (e - 1) * C]
 
-        def slots_of(e):
-            return slice(e * C, (e + 1) * C)
+        def sums_tile(first, count, tag):
+            pair = keep.tile([P, count, 2, C], F32, name="y%d" % first, tag=tag)
+            for j in range(count):
+                ys[first + j] = pair[:, j, :, :]
 
-        def weigh_first(u):
-            nc.vector.tensor_tensor(
-                out=y_first[u][:], in0=acc_first[u][:], in1=gate_of(0)[:, 2 * u : 2 * u + 2, :], op=MULT
-            )
+        def empty_bank(u):
+            nc.scalar.copy(out=ys[u], in_=accs[u][:])
 
-        def empty_bank(e, tag):
-            y_raw = keep.tile([P, NB, C], F32, name="y_raw%d" % e, tag=tag)
-            nc.scalar.copy(out=y_raw[:], in_=accs[e][:])
-            y_raws[e] = y_raw
+        def weigh_and_scatter(u):
+            e = u // 2
+            for i in range(2):
+                b = 2 * (u % 2) + i
+                nc.vector.tensor_tensor(
+                    out=windows[b][:].indirect(offsets[:, e * (C // 16) : (e + 1) * (C // 16)]),
+                    in0=ys[u][:, i, :],
+                    in1=gate_of(e, b),
+                    op=MULT,
+                )
+                if e == E - 1:
+                    nc.sync.dma_start(out[b * P : (b + 1) * P, :], windows[b][:])
 
-        def offsets_of(e):
-            return offsets[:, e * (C // 16) : (e + 1) * (C // 16)]
-
-        def scatter_weighed(e, b):
-            nc.vector.tensor_copy(windows[b][:].indirect(offsets_of(e)), y_first[b // 2][:, b % 2, :])
-
-        def weigh_and_scatter(e, b):
-            nc.vector.tensor_tensor(
-                out=windows[b][:].indirect(offsets_of(e)), in0=y_raws[e][:, b, :], in1=gate_of(e)[:, b, :], op=MULT
-            )
-
-        H = N // 2
         gather(0)
-        interleave_x(nc.scalar.copy, 0)
+        nc.vector.tensor_copy(
+            out=g4s[1][:, :, 0:1], in_=g4s[0][:, PACK - 1, 0:PACK].rearrange("p (t o) -> p t o", o=1)
+        )
         gather(1)
-        interleave_w(nc.vector.tensor_copy, 0, 0, H)
+        interleave_x(nc.scalar.copy, 0, "xg0")
         quantize_x(0)
-        interleave_w(nc.vector.tensor_copy, 0, H, N)
-        quantize_w(0, 0, H)
-        multiply(0, (0, 1))
-        quantize_w(0, H, N)
-        multiply(0, (2, 3))
-        interleave_x(nc.scalar.copy, 1)
-        quantize_x(1)
-        interleave_w(nc.scalar.copy, 1, 0, H)
-        interleave_w(nc.scalar.copy, 1, H, N)
-        weigh_first(0)
-        scatter_weighed(0, 0)
-        weigh_first(1)
-        scatter_weighed(0, 1)
+        interleave_w(nc.scalar.copy, 0, "first")
+        quantize_w(0)
+        multiply(0)
+        sums_tile(0, 1, "y0")
+        empty_bank(0)
+        interleave_w(nc.vector.tensor_copy, 1, "first")
         quantize_w(1)
         multiply(1)
-        interleave_w(nc.scalar.copy, 2, 0, H)
-        interleave_w(nc.scalar.copy, 2, H, N)
-        empty_bank(1, "raw2")
-        scatter_weighed(0, 2)
-        quantize_w(2)
-        multiply(2)
-        interleave_w(nc.scalar.copy, 3, 0, H)
-        interleave_w(nc.scalar.copy, 3, H, N)
-        empty_bank(2, "raw3")
-        scatter_weighed(0, 3)
-        weigh_and_scatter(1, 0)
-        quantize_w(3)
-        multiply(3)
-        empty_bank(3, "raw0")
-        for b in (1, 2, 3):
-            weigh_and_scatter(1, b)
-        for b in range(NB):
-            weigh_and_scatter(2, b)
-        for b in range(NB):
-            weigh_and_scatter(3, b)
-            nc.sync.dma_start(out[b * P : (b + 1) * P, :], windows[b][:])
+        interleave_x(nc.vector.tensor_copy, 1, "first")
+        weigh_and_scatter(0)
+        quantize_x(1)
+        for e in range(1, E):
+            for u in (2 * e, 2 * e + 1):
+                interleave_w(nc.scalar.copy, u, "wg%d" % u)
+                quantize_w(u)
+                multiply(u)
+            sums_tile(2 * e - 1, 2, "raw%d" % e)
+            for u in (2 * e - 1, 2 * e):
+                empty_bank(u)
+                weigh_and_scatter(u)
+        sums_tile(UNITS - 1, 1, "y7")
+        empty_bank(UNITS - 1)
+        weigh_and_scatter(UNITS - 1)

@@ -42,7 +42,7 @@ def tile_routed_moe_kernel(tc, xT, w, gate, offs, out):
 
         w_view = w.rearrange("e (p t) n -> e p t n", t=PACK)
         gate_view = gate.rearrange("(b p) j -> p b j", p=P)
-        w_raw = [keep.tile([P, PACK, N], F32, name="w_raw%d" % e, tag="raw%d" % e) for e in range(E)]
+        w_raw = [keep.tile([P, PACK, N], F32, name="w_raw%d" % e) for e in range(E)]
         gate_a = [keep.tile([P, NB, C], F32, name="gate_a%d" % e) for e in range(2)]
         gate_b = keep.tile([P, NB, HALF], F32, name="gate_b")
         for t in range(PACK):
@@ -120,13 +120,9 @@ def tile_routed_moe_kernel(tc, xT, w, gate, offs, out):
                 return gate_a[e][:, b, :]
             return gate_b[:, b, (e - 2) * C : (e - 1) * C]
 
-        def sums_tile(first, count, tag):
-            pair = keep.tile([P, count, 2, C], F32, name="y%d" % first, tag=tag)
-            for j in range(count):
-                ys[first + j] = pair[:, j, :, :]
-
         def empty_bank(u):
-            nc.scalar.copy(out=ys[u], in_=accs[u][:])
+            ys[u] = keep.tile([P, 2, C], F32, name="y%d" % u)
+            nc.scalar.copy(out=ys[u][:], in_=accs[u][:])
 
         def weigh_and_scatter(u):
             e = u // 2
@@ -151,23 +147,19 @@ def tile_routed_moe_kernel(tc, xT, w, gate, offs, out):
         interleave_w(nc.scalar.copy, 0, "first")
         quantize_w(0)
         multiply(0)
-        sums_tile(0, 1, "y0")
         empty_bank(0)
         interleave_w(nc.vector.tensor_copy, 1, "first")
         quantize_w(1)
         multiply(1)
-        interleave_x(nc.vector.tensor_copy, 1, "first")
         weigh_and_scatter(0)
-        quantize_x(1)
-        for e in range(1, E):
-            for u in (2 * e, 2 * e + 1):
-                interleave_w(nc.scalar.copy, u, "wg%d" % u)
-                quantize_w(u)
-                multiply(u)
-            sums_tile(2 * e - 1, 2, "raw%d" % e)
-            for u in (2 * e - 1, 2 * e):
-                empty_bank(u)
-                weigh_and_scatter(u)
-        sums_tile(UNITS - 1, 1, "y7")
+        for u in range(2, UNITS):
+            if u == 4:
+                interleave_x(nc.scalar.copy, 1, "wg3")
+                quantize_x(1)
+            interleave_w(nc.scalar.copy, u, "wg%d" % u)
+            quantize_w(u)
+            multiply(u)
+            empty_bank(u - 1)
+            weigh_and_scatter(u - 1)
         empty_bank(UNITS - 1)
         weigh_and_scatter(UNITS - 1)

@@ -65,11 +65,10 @@ def tile_routed_moe_kernel(tc, xT, w, gate, offs, out):
         w_grouped = {}
         ys = {}
 
-        def gather(h):
-            for t in range(PACK):
-                nc.vector.tensor_copy(
-                    g4s[h][:, t, :], planes[t][:].indirect(offsets[:, h * (HALF // 16) : (h + 1) * (HALF // 16)])
-                )
+        def gather(h, t):
+            nc.vector.tensor_copy(
+                g4s[h][:, t, :], planes[t][:].indirect(offsets[:, h * (HALF // 16) : (h + 1) * (HALF // 16)])
+            )
 
         def interleave_x(engine_copy, h, tag):
             x_grouped[h] = keep.tile([P, HALF, PACK], BF16, name="xg%d" % h, tag=tag, align_bytes=64)
@@ -137,24 +136,37 @@ def tile_routed_moe_kernel(tc, xT, w, gate, offs, out):
                 if e == E - 1:
                     nc.sync.dma_start(out[b * P : (b + 1) * P, :], windows[b][:])
 
-        gather(0)
+        for t in range(PACK - 1):
+            gather(0, t)
         nc.vector.tensor_copy(
-            out=g4s[1][:, :, 0:1], in_=g4s[0][:, PACK - 1, 0:PACK].rearrange("p (t o) -> p t o", o=1)
+            out=g4s[1][:, :, 0:1], in_=planes[PACK - 1][:, 0:PACK].rearrange("p (t o) -> p t o", o=1)
         )
-        gather(1)
+        gather(0, PACK - 1)
+        for t in range(PACK):
+            gather(1, t)
         interleave_x(nc.scalar.copy, 0, "xg0")
         quantize_x(0)
-        interleave_w(nc.scalar.copy, 0, "first")
+        interleave_w(nc.scalar.copy, 0, "wg0")
         quantize_w(0)
         multiply(0)
+        w_grouped[1] = keep.tile([P, H, PACK], BF16, name="wg1", align_bytes=64)
+        nc.scalar.copy(out=w_grouped[1][:, 0:1, :], in_=w_grouped[0][:, 0:1, :])
         empty_bank(0)
-        interleave_w(nc.vector.tensor_copy, 1, "first")
+        nc.vector.tensor_copy(
+            out=w_grouped[1][:].rearrange("p (c i) t -> p c t i", i=4),
+            in_=w_raw[0][:, :, H:N].rearrange("p t (c i) -> p c t i", i=4),
+        )
         quantize_w(1)
         multiply(1)
         weigh_and_scatter(0)
         for u in range(2, UNITS):
             if u == 4:
-                interleave_x(nc.scalar.copy, 1, "wg3")
+                x_grouped[1] = keep.tile([P, HALF, PACK], BF16, name="xg1", align_bytes=64)
+                nc.scalar.copy(out=x_grouped[1][:, 0:1, :], in_=w_grouped[3][:, 0:1, :])
+                nc.scalar.copy(
+                    out=x_grouped[1][:].rearrange("p (c i) t -> p c t i", i=4),
+                    in_=g4s[1][:].rearrange("p t (c i) -> p c t i", i=4),
+                )
                 quantize_x(1)
             interleave_w(nc.scalar.copy, u, "wg%d" % u)
             quantize_w(u)

@@ -149,15 +149,10 @@ def tile_routed_moe_kernel(tc, xT, w, gate, offs, out):
         interleave_w(nc.scalar.copy, 0, "wg0")
         quantize_w(0)
         multiply(0)
-        w_grouped[1] = keep.tile([P, H, PACK], BF16, name="wg1", align_bytes=64)
-        nc.scalar.copy(out=w_grouped[1][:, 0:1, :], in_=w_grouped[0][:, 0:1, :])
-        empty_bank(0)
-        nc.vector.tensor_copy(
-            out=w_grouped[1][:].rearrange("p (c i) t -> p c t i", i=4),
-            in_=w_raw[0][:, :, H:N].rearrange("p t (c i) -> p c t i", i=4),
-        )
+        interleave_w(nc.scalar.copy, 1, "wg1")
         quantize_w(1)
         multiply(1)
+        empty_bank(0)
         weigh_and_scatter(0)
         for u in range(2, UNITS):
             if u == 4:

@@ -45,8 +45,7 @@ def tile_routed_moe_kernel(tc, xT, w, gate, offs, out):
         w_raw = [keep.tile([P, PACK, N], F32, name="w_raw%d" % e) for e in range(E)]
         gate_a = [keep.tile([P, NB, C], F32, name="gate_a%d" % e) for e in range(2)]
         gate_b = keep.tile([P, NB, HALF], F32, name="gate_b")
-        for t in range(PACK):
-            nc.sync.dma_start(w_raw[0][:, t, :], w_view[0][:, t, :])
+        nc.sync.dma_start(w_raw[0][:], w_view[0])
         nc.sync.dma_start(gate_a[0][:], gate_view[:, :, 0:C])
         nc.sync.dma_start(w_raw[1][:], w_view[1])
         nc.sync.dma_start(w_raw[2][:], w_view[2])

@@ -72,16 +72,16 @@ def tile_routed_moe_kernel(tc, xT, w, gate, offs, out):
         def interleave_x(engine_copy, h, tag):
             x_grouped[h] = keep.tile([P, HALF, PACK], BF16, name="xg%d" % h, tag=tag, align_bytes=64)
             engine_copy(
-                out=x_grouped[h][:].rearrange("p (c i) t -> p c t i", i=4),
-                in_=g4s[h][:].rearrange("p t (c i) -> p c t i", i=4),
+                out=x_grouped[h][:].rearrange("p (c i) t -> p c t i", i=8),
+                in_=g4s[h][:].rearrange("p t (c i) -> p c t i", i=8),
             )
 
         def interleave_w(engine_copy, u, tag):
             e, c0 = u // 2, (u % 2) * H
             w_grouped[u] = keep.tile([P, H, PACK], BF16, name="wg%d" % u, tag=tag, align_bytes=64)
             engine_copy(
-                out=w_grouped[u][:].rearrange("p (c i) t -> p c t i", i=4),
-                in_=w_raw[e][:, :, c0 : c0 + H].rearrange("p t (c i) -> p c t i", i=4),
+                out=w_grouped[u][:].rearrange("p (c i) t -> p c t i", i=8),
+                in_=w_raw[e][:, :, c0 : c0 + H].rearrange("p t (c i) -> p c t i", i=8),
             )
 
         def quantize_w(u):
@@ -158,8 +158,8 @@ def tile_routed_moe_kernel(tc, xT, w, gate, offs, out):
                 x_grouped[1] = keep.tile([P, HALF, PACK], BF16, name="xg1", align_bytes=64)
                 nc.scalar.copy(out=x_grouped[1][:, 0:1, :], in_=w_grouped[3][:, 0:1, :])
                 nc.scalar.copy(
-                    out=x_grouped[1][:].rearrange("p (c i) t -> p c t i", i=4),
-                    in_=g4s[1][:].rearrange("p t (c i) -> p c t i", i=4),
+                    out=x_grouped[1][:].rearrange("p (c i) t -> p c t i", i=8),
+                    in_=g4s[1][:].rearrange("p t (c i) -> p c t i", i=8),
                 )
                 quantize_x(1)
             interleave_w(nc.scalar.copy, u, "wg%d" % u)

@@ -31,7 +31,6 @@ def tile_routed_moe_kernel(tc, xT, w, gate, offs, out):
         psum = ctx.enter_context(tc.psum_pool(name="psum", bufs=1))
 
         offsets = lists.tile([P, S // 16], U16, name="offsets")
-        nc.sync.dma_start(offsets[:], offs)
 
         x_view = xT.rearrange("(p t) n -> p t n", t=PACK)
         planes = []
@@ -39,6 +38,8 @@ def tile_routed_moe_kernel(tc, xT, w, gate, offs, out):
             plane = keep.tile([P, T], F32, name="plane%d" % t)
             nc.sync.dma_start(plane[:], x_view[:, t, :])
             planes.append(plane)
+            if t == 0:
+                nc.sync.dma_start(offsets[:], offs)
 
         w_view = w.rearrange("e (p t) n -> e p t n", t=PACK)
         gate_view = gate.rearrange("(b p) j -> p b j", p=P)
@@ -119,8 +120,14 @@ def tile_routed_moe_kernel(tc, xT, w, gate, offs, out):
             return gate_b[:, b, (e - 2) * C : (e - 1) * C]
 
         def empty_bank(u):
-            ys[u] = keep.tile([P, 2, C], F32, name="y%d" % u)
-            nc.scalar.copy(out=ys[u][:], in_=accs[u][:])
+            if u == 0:
+                ys[u] = [keep.tile([P, C], F32, name="y0_%d" % i) for i in range(2)]
+                for i in range(2):
+                    nc.scalar.copy(out=ys[u][i][:], in_=accs[u][:, i, :])
+            else:
+                whole = keep.tile([P, 2, C], F32, name="y%d" % u)
+                nc.scalar.copy(out=whole[:], in_=accs[u][:])
+                ys[u] = [whole[:, i, :] for i in range(2)]
 
         def weigh_and_scatter(u):
             e = u // 2
@@ -128,7 +135,7 @@ def tile_routed_moe_kernel(tc, xT, w, gate, offs, out):
                 b = 2 * (u % 2) + i
                 nc.vector.tensor_tensor(
                     out=windows[b][:].indirect(offsets[:, e * (C // 16) : (e + 1) * (C // 16)]),
-                    in0=ys[u][:, i, :],
+                    in0=ys[u][i][:] if u == 0 else ys[u][i],
                     in1=gate_of(e, b),
                     op=MULT,
                 )

@@ -144,7 +144,7 @@ def tile_routed_moe_kernel(tc, xT, w, gate, offs, out):
 
         for t in range(PACK - 1):
             gather(0, t)
-        nc.vector.tensor_copy(
+        nc.gpsimd.tensor_copy(
             out=g4s[1][:, :, 0:1], in_=planes[PACK - 1][:, 0:PACK].rearrange("p (t o) -> p t o", o=1)
         )
         gather(0, PACK - 1)

from contextlib import ExitStack

import concourse.mybir as mybir

K, T, E, C, N = 512, 512, 4, 128, 512
FLOPS = 2 * K * N * E * C

F32 = mybir.dt.float32
BF16 = mybir.dt.bfloat16
U32 = mybir.dt.uint32
U16 = mybir.dt.uint16
U8 = mybir.dt.uint8
FP8X4 = mybir.dt.float8_e4m3fn_x4
MULT = mybir.AluOpType.mult
ADD = mybir.AluOpType.add

P = 128
PACK = 4
NB = N // P
S = E * C
HALF = 256
H = N // 2
UNITS = 2 * E


def tile_routed_moe_kernel(tc, xT, w, gate, offs, out):
    nc = tc.nc
    with ExitStack() as ctx:
        lists = ctx.enter_context(tc.tile_pool(name="lists", bufs=1))
        keep = ctx.enter_context(tc.tile_pool(name="keep", bufs=1))
        psum = ctx.enter_context(tc.psum_pool(name="psum", bufs=1))

        offsets = lists.tile([P, S // 16], U16, name="offsets")

        x_view = xT.rearrange("(p t) n -> p t n", t=PACK)
        planes = []
        for t in range(PACK):
            plane = keep.tile([P, T], F32, name="plane%d" % t)
            nc.sync.dma_start(plane[:], x_view[:, t, :])
            planes.append(plane)
            if t == 0:
                nc.sync.dma_start(offsets[:], offs)

        w_view = w.rearrange("e (p t) n -> e p t n", t=PACK)
        gate_view = gate.rearrange("(b p) j -> p b j", p=P)
        w_raw = [keep.tile([P, PACK, N], F32, name="w_raw%d" % e) for e in range(E)]
        gate_a = [keep.tile([P, NB, C], F32, name="gate_a%d" % e) for e in range(2)]
        gate_b = keep.tile([P, NB, HALF], F32, name="gate_b")
        nc.sync.dma_start(w_raw[0][:], w_view[0])
        nc.sync.dma_start(gate_a[0][:], gate_view[:, :, 0:C])
        nc.sync.dma_start(w_raw[1][:], w_view[1])
        nc.sync.dma_start(w_raw[2][:], w_view[2])
        nc.sync.dma_start(gate_a[1][:], gate_view[:, :, C : 2 * C])
        nc.sync.dma_start(w_raw[3][:], w_view[3])
        nc.sync.dma_start(gate_b[:], gate_view[:, :, HALF:S])

        x_codes = [keep.tile([P, HALF], U32, name="x_codes%d" % h, align_bytes=64) for h in range(2)]
        x_scales = [keep.tile([P, HALF], U8, name="x_scales%d" % h, align_bytes=64) for h in range(2)]
        windows = [keep.tile([P, T], F32, name="window%d" % b) for b in range(NB)]
        g4s = [keep.tile([P, PACK, HALF], F32, name="g4_%d" % h) for h in range(2)]
        w_codes = [keep.tile([P, H], U32, name="w_codes%d" % u, align_bytes=64) for u in range(UNITS)]
        w_scales = [keep.tile([P, H], U8, name="w_scales%d" % u, align_bytes=64) for u in range(UNITS)]
        accs = [psum.tile([P, 2, C], F32, name="acc%d" % u) for u in range(UNITS)]
        x_grouped = {}
        w_grouped = {}
        ys = {}

        def gather(h, t):
            nc.vector.tensor_copy(
                g4s[h][:, t, :], planes[t][:].indirect(offsets[:, h * (HALF // 16) : (h + 1) * (HALF // 16)])
            )

        def interleave_x(engine_copy, h, tag):
            x_grouped[h] = keep.tile([P, HALF, PACK], BF16, name="xg%d" % h, tag=tag, align_bytes=64)
            engine_copy(
                out=x_grouped[h][:].rearrange("p (c i) t -> p c t i", i=8),
                in_=g4s[h][:].rearrange("p t (c i) -> p c t i", i=8),
            )

        def interleave_w(engine_copy, u, tag):
            e, c0 = u // 2, (u % 2) * H
            w_grouped[u] = keep.tile([P, H, PACK], BF16, name="wg%d" % u, tag=tag, align_bytes=64)
            engine_copy(
                out=w_grouped[u][:].rearrange("p (c i) t -> p c t i", i=8),
                in_=w_raw[e][:, :, c0 : c0 + H].rearrange("p t (c i) -> p c t i", i=8),
            )

        def quantize_w(u):
            nc.vector.quantize_mx(
                out=w_codes[u][:].bitcast(FP8X4),
                scales=w_scales[u][:],
                in_=w_grouped[u][:].rearrange("p n t -> p (n t)"),
            )

        def quantize_x(h):
            nc.vector.quantize_mx(
                out=x_codes[h][:].bitcast(FP8X4),
                scales=x_scales[h][:],
                in_=x_grouped[h][:].rearrange("p c t -> p (c t)"),
            )

        def multiply(u):
            e = u // 2
            slots = slice((e % 2) * C, (e % 2 + 1) * C)
            for i in range(2):
                feats = slice(i * P, (i + 1) * P)
                nc.tensor.matmul_mx(
                    out=accs[u][:, i, :],
                    lhsT=w_codes[u][:, feats].bitcast(FP8X4),
                    lhsT_scale=w_scales[u][:, feats],
                    rhs=x_codes[e // 2][:, slots].bitcast(FP8X4),
                    rhs_scale=x_scales[e // 2][:, slots],
                    start=True,
                    stop=True,
                )

        def gate_of(e, b):
            if e < 2:
                return gate_a[e][:, b, :]
            return gate_b[:, b, (e - 2) * C : (e - 1) * C]

        def empty_bank(u):
            if u == 0:
                ys[u] = [keep.tile([P, C], F32, name="y0_%d" % i) for i in range(2)]
                for i in range(2):
                    nc.scalar.copy(out=ys[u][i][:], in_=accs[u][:, i, :])
            else:
                whole = keep.tile([P, 2, C], F32, name="y%d" % u)
                nc.scalar.copy(out=whole[:], in_=accs[u][:])
                ys[u] = [whole[:, i, :] for i in range(2)]

        def weigh_and_scatter(u):
            e = u // 2
            for i in range(2):
                b = 2 * (u % 2) + i
                nc.vector.tensor_tensor(
                    out=windows[b][:].indirect(offsets[:, e * (C // 16) : (e + 1) * (C // 16)]),
                    in0=ys[u][i][:] if u == 0 else ys[u][i],
                    in1=gate_of(e, b),
                    op=MULT,
                )
                if e == E - 1:
                    nc.sync.dma_start(out[b * P : (b + 1) * P, :], windows[b][:])

        for t in range(PACK - 1):
            gather(0, t)
        nc.gpsimd.tensor_copy(
            out=g4s[1][:, :, 0:1], in_=planes[PACK - 1][:, 0:PACK].rearrange("p (t o) -> p t o", o=1)
        )
        gather(0, PACK - 1)
        for t in range(PACK):
            gather(1, t)
        interleave_x(nc.scalar.copy, 0, "xg0")
        quantize_x(0)
        interleave_w(nc.scalar.copy, 0, "wg0")
        quantize_w(0)
        multiply(0)
        interleave_w(nc.scalar.copy, 1, "wg1")
        quantize_w(1)
        multiply(1)
        empty_bank(0)
        weigh_and_scatter(0)
        for u in range(2, UNITS):
            if u == 4:
                x_grouped[1] = keep.tile([P, HALF, PACK], BF16, name="xg1", align_bytes=64)
                nc.scalar.copy(out=x_grouped[1][:, 0:1, :], in_=w_grouped[3][:, 0:1, :])
                nc.scalar.copy(
                    out=x_grouped[1][:].rearrange("p (c i) t -> p c t i", i=8),
                    in_=g4s[1][:].rearrange("p t (c i) -> p c t i", i=8),
                )
                quantize_x(1)
            interleave_w(nc.scalar.copy, u, "wg%d" % u)
            quantize_w(u)
            multiply(u)
            empty_bank(u - 1)
            weigh_and_scatter(u - 1)
        empty_bank(UNITS - 1)
        weigh_and_scatter(UNITS - 1)
